import numpy as np
import ml_dtypes


def mxq(x, axis, fmt="e4m3"):
    dtype, down = {"e4m3": (ml_dtypes.float8_e4m3fn, 7), "e5m2": (ml_dtypes.float8_e5m2, 14)}[fmt]
    v = np.moveaxis(np.asarray(x, np.float32).astype(ml_dtypes.bfloat16).astype(np.float64), axis, -1)
    blocks = v.reshape(v.shape[:-1] + (-1, 32))
    amax = np.abs(blocks).max(-1, keepdims=True)
    byte = np.maximum(np.where(amax > 0, np.frexp(amax)[1] - 1 + 127, 0) - down, 1)
    scale = np.exp2(byte - 127.0)
    codes = (blocks / scale).astype(np.float32).astype(dtype).astype(np.float64)
    return np.moveaxis((codes * scale).reshape(v.shape), -1, axis)


WIDE = False


def mx_kscale(k):
    if not WIDE:
        return np.ones(k)
    levels = np.array([10, -10, 5, -5, 0])
    if k % 512:
        return np.exp2(np.random.permutation(np.resize(levels, k // 32))).repeat(32)
    a = np.empty((k // 512, 16))
    for p in range(k // 512):
        a[p, :8] = np.random.permutation(np.resize(levels, 8))
        for g in range(8):
            far = levels[np.abs(levels - a[p, g]) >= 10]
            a[p, g + 8] = far[np.random.randint(len(far))]
    return np.exp2(a.ravel()).repeat(32)


def f64(x):
    return np.asarray(x).astype(np.float64)


def striped(idx):
    return np.tile(idx.reshape(-1, 16).T, (8, 1)).astype(np.uint16)


def unstriped(offs):
    return offs[:16].T.reshape(-1).astype(np.int64)


def pack_weight(w):
    k, n = w.shape
    w = f64(np.asarray(w, np.float32).astype(ml_dtypes.bfloat16)).reshape(k // 32, 32, n)
    amax = np.abs(w).max(1)
    byte = np.clip(np.where(amax > 0, np.frexp(amax)[1] - 1 + 127 - 7, 1), 1, 254)
    scaled = (w * np.exp2(127.0 - byte)[:, None, :]).reshape(k, n).astype(np.float32)
    words = np.ascontiguousarray(scaled.reshape(k // 512, 128, 4, n).transpose(0, 1, 3, 2)).astype(ml_dtypes.float8_e4m3fn).view(np.uint8)
    return words, np.ascontiguousarray(byte.astype(np.uint8).reshape(k // 512, 16, n))


def unpack_weight(words, scales):
    g, p, n, _ = words.shape
    vals = np.ascontiguousarray(words).view(ml_dtypes.float8_e4m3fn).astype(np.float64) * np.repeat(np.exp2(scales.astype(np.float64) - 127.0), 8, axis=1)[..., None]
    return vals.transpose(0, 1, 3, 2).reshape(g * 512, n)


def relu(v):
    return np.maximum(v, 0.0)


K, T, S, V, H, G = 1024, 1024, 512, 512, 512, 2048


def setup_inputs():
    n = np.random.standard_normal
    s = mx_kscale(K)[:, None]
    u = mx_kscale(H)
    packed_xT = pack_weight(n((K, T)) * s)
    packed_vT = pack_weight(n((H, G)) / np.sqrt(H) / u[:, None])
    return {
        "x_words": packed_xT[0],
        "x_scales": packed_xT[1],
        "w1": (n((K, H)) / np.sqrt(K) / s * u).astype(np.float32),
        "v_words": packed_vT[0],
        "v_scales": packed_vT[1],
        "offs": striped(np.random.permutation(T)[:S]),
        "neg": striped(np.random.permutation(G)[:V]),
    }


def reference(x_words, x_scales, w1, v_words, v_scales, offs, neg):
    xq = unpack_weight(x_words, x_scales)[:, unstriped(offs)]
    h = relu(mxq(f64(w1), 0, "e4m3").T @ xq)
    v_neg = unpack_weight(v_words, v_scales)[:, unstriped(neg)]
    y = mxq(h, 0, "e4m3").T @ v_neg
    e = np.exp(y - y.max(axis=1, keepdims=True))
    return e / e.sum(axis=1, keepdims=True)

@@ -1,0 +1,168 @@
+from contextlib import ExitStack
+
+import concourse.mybir as mybir
+
+K, T, S, V, H, G = 1024, 1024, 512, 512, 512, 2048
+FLOPS = 2 * K * H * S + 2 * H * S * V
+
+F32 = mybir.dt.float32
+BF16 = mybir.dt.bfloat16
+I32 = mybir.dt.int32
+U32 = mybir.dt.uint32
+U16 = mybir.dt.uint16
+U8 = mybir.dt.uint8
+FP8X4 = mybir.dt.float8_e4m3fn_x4
+ACT = mybir.ActivationFunctionType
+ALU = mybir.AluOpType
+
+P = 128
+PACK = 4
+QUADS = 4
+CHUNK = 128
+CHUNKS = S // CHUNK
+LIST_COLS = CHUNK // 16
+VECTOR_SHARE = 80
+V_PLANE = 8
+
+
+def tile_picked_zmoco_relu_p_kernel(
+    tc, x_words, x_scales, w1, v_words, v_scales, offs, neg, out
+):
+    nc = tc.nc
+    with ExitStack() as ctx:
+        lists = ctx.enter_context(tc.tile_pool(name="lists", bufs=1))
+        sb = ctx.enter_context(tc.tile_pool(name="sb", bufs=1))
+        turns = ctx.enter_context(tc.tile_pool(name="turns", bufs=1))
+        psum = ctx.enter_context(tc.psum_pool(name="psum", bufs=1))
+
+        def words_of(table, o):
+            return table[o].rearrange("p n r -> p (n r)").bitcast(I32)
+
+        def load_w(o):
+            raw = sb.tile([P, PACK, H], F32, name=f"w_raw{o}")
+            nc.sync.dma_start(raw[:], w1[512 * o : 512 * (o + 1), :].rearrange("(p r) i -> p r i", r=PACK))
+            return raw
+
+        x_bytes = turns.tile([P, T], U8, name="x_bytes", align_bytes=64, offset=0)
+        nc.gpsimd.memset(x_bytes[:].bitcast(I32), 0)
+        v_bytes = turns.tile([P, G], U8, name="v_bytes", align_bytes=64, offset=T)
+        nc.vector.memset(v_bytes[:].bitcast(I32), 0)
+
+        offs_sb = lists.tile([P, S // 16], U16, name="offs_sb")
+        nc.sync.dma_start(offs_sb[:], offs)
+        x_table0 = sb.tile([P, T], I32, name="x_table0", tag="table", align_bytes=64)
+        nc.sync.dma_start(x_table0[:], words_of(x_words, 0))
+        neg_sb = lists.tile([P, V // 16], U16, name="neg_sb")
+        nc.sync.dma_start(neg_sb[:], neg)
+        w_raw = [load_w(0), load_w(1)]
+        x_table1 = sb.tile([P, T], I32, name="x_table1", align_bytes=64)
+        nc.sync.dma_start(x_table1[:], words_of(x_words, 1))
+
+        for q in range(QUADS):
+            nc.scalar.dma_start(
+                v_bytes[32 * q + V_PLANE : 32 * q + V_PLANE + 4, :].bitcast(I32),
+                v_scales[0, 4 * q : 4 * q + 4, :].bitcast(I32),
+            )
+        for q in range(QUADS):
+            (nc.gpsimd if q < 3 else nc.scalar).dma_start(
+                x_bytes[32 * q : 32 * q + 8, :].bitcast(I32), x_scales[:, 4 * q : 4 * q + 4, :].bitcast(I32)
+            )
+
+        x_codes = [sb.tile([P, S], U32, name=f"x_codes{o}", align_bytes=64) for o in range(2)]
+        x_scale = sb.tile([P, S], U8, name="x_scale", align_bytes=64)
+        v_codes = sb.tile([P, V], U32, name="v_codes", align_bytes=64)
+        v_scale = sb.tile([P, V], U8, name="v_scale", align_bytes=64)
+        nc.vector.tensor_copy(x_codes[0][:], x_table0[:].bitcast(U32).indirect(offs_sb[:]))
+        v_table = sb.tile([P, G], I32, name="v_table", tag="table", align_bytes=64)
+        nc.sync.dma_start(v_table[:], words_of(v_words, 0))
+        nc.vector.tensor_copy(v_scale[:], v_bytes[:].indirect(neg_sb[:]))
+        nc.vector.tensor_copy(x_scale[:], x_bytes[:].indirect(offs_sb[:]))
+
+        w_bf = [
+            sb.tile([P, PACK, P, PACK], BF16, name="w_bf0", align_bytes=64),
+            turns.tile([P, PACK, P, PACK], BF16, name="w_bf1", align_bytes=64, offset=0),
+        ]
+        w_codes = [sb.tile([P, H], U32, name=f"w_codes{o}", align_bytes=64) for o in range(2)]
+        w_scale = [sb.tile([P, H], U8, name=f"w_scale{o}", align_bytes=64) for o in range(2)]
+        src = [w_raw[o][:].rearrange("p r (m j) -> p m r j", j=PACK) for o in range(2)]
+        dst = [w_bf[o][:].rearrange("p j m r -> p m r j") for o in range(2)]
+
+        def quantize_w(o, j0, j1):
+            cols = slice(P * j0, P * j1)
+            nc.vector.quantize_mx(
+                out=w_codes[o][:, cols].bitcast(FP8X4),
+                scales=w_scale[o][:, cols],
+                in_=w_bf[o][:, j0:j1].rearrange("p j m r -> p (j m r)"),
+            )
+
+        def gather_x1(c):
+            nc.vector.tensor_copy(
+                x_codes[1][:, CHUNK * c : CHUNK * (c + 1)],
+                x_table1[:].bitcast(U32).indirect(offs_sb[:, LIST_COLS * c : LIST_COLS * (c + 1)]),
+            )
+
+        nc.scalar.activation(dst[0], src[0], ACT.Copy)
+        nc.vector.tensor_copy(dst[1][:, :VECTOR_SHARE], src[1][:, :VECTOR_SHARE])
+        nc.scalar.activation(dst[1][:, VECTOR_SHARE:], src[1][:, VECTOR_SHARE:], ACT.Copy)
+        quantize_w(0, 0, PACK)
+        gather_x1(0)
+        quantize_w(1, 0, 2)
+        quantize_w(1, 2, 4)
+        for c in range(1, CHUNKS):
+            gather_x1(c)
+
+        h_bf = []
+        for c in range(CHUNKS):
+            cols = slice(CHUNK * c, CHUNK * (c + 1))
+            h_acc = psum.tile([P, PACK, CHUNK], F32, name=f"h_acc{c}")
+            for j in range(PACK):
+                for o in range(2):
+                    nc.tensor.matmul_mx(
+                        out=h_acc[:, j, :],
+                        lhsT=w_codes[o][:, P * j : P * (j + 1)].bitcast(FP8X4),
+                        lhsT_scale=w_scale[o][:, P * j : P * (j + 1)],
+                        rhs=x_codes[o][:, cols].bitcast(FP8X4),
+                        rhs_scale=x_scale[4 * o :, cols],
+                        start=(o == 0),
+                        stop=(o == 1),
+                    )
+            h_bf.append(sb.tile([P, CHUNK, PACK], BF16, name=f"h_bf{c}", align_bytes=64))
+            nc.scalar.activation(h_bf[c][:], h_acc[:].rearrange("p j t -> p t j"), ACT.Relu)
+
+        h_codes = [sb.tile([P, CHUNK], U32, name=f"h_codes{c}", align_bytes=64) for c in range(CHUNKS)]
+        h_scale = [sb.tile([P, CHUNK], U8, name=f"h_scale{c}", align_bytes=64) for c in range(CHUNKS)]
+
+        def quantize_h(c):
+            nc.vector.quantize_mx(
+                out=h_codes[c][:].bitcast(FP8X4),
+                scales=h_scale[c][:],
+                in_=h_bf[c][:].rearrange("p t j -> p (t j)"),
+            )
+
+        nc.vector.tensor_copy(v_codes[:], v_table[:].bitcast(U32).indirect(neg_sb[:]))
+        for c in range(CHUNKS):
+            quantize_h(c)
+
+        e = [sb.tile([P, V], F32, name=f"e{c}") for c in range(CHUNKS)]
+        total = [sb.tile([P, 1], F32, name=f"total{c}") for c in range(CHUNKS)]
+        for c in range(CHUNKS):
+            y_acc = psum.tile([P, V], F32, name=f"y_acc{c}")
+            nc.tensor.matmul_mx(
+                out=y_acc[:],
+                lhsT=h_codes[c][:].bitcast(FP8X4),
+                lhsT_scale=h_scale[c][:],
+                rhs=v_codes[:].bitcast(FP8X4),
+                rhs_scale=v_scale[V_PLANE:, :],
+                start=True,
+                stop=True,
+            )
+            neg_max = sb.tile([P, 1], F32, name=f"neg_max{c}")
+            nc.vector.tensor_reduce(neg_max[:], y_acc[:], mybir.AxisListType.X, ALU.max, negate=True)
+            nc.scalar.activation(e[c][:], y_acc[:], ACT.Exp, bias=neg_max[:], scale=1.0, accum_out=total[c][:])
+
+        for c in range(CHUNKS):
+            inv = sb.tile([P, 1], F32, name=f"inv{c}")
+            nc.vector.reciprocal(inv[:], total[c][:])
+            prob = sb.tile([P, V], F32, name=f"prob{c}")
+            nc.vector.tensor_scalar(prob[:], e[c][:], inv[:], None, ALU.mult)
+            nc.sync.dma_start(out[CHUNK * c : CHUNK * (c + 1), :], prob[:])

@@ -21,7 +21,7 @@ QUADS = 4
 CHUNK = 128
 CHUNKS = S // CHUNK
 LIST_COLS = CHUNK // 16
-VECTOR_SHARE = 80
+VECTOR_SHARE = (48, 88)
 V_PLANE = 8
 
 
@@ -44,38 +44,36 @@ def tile_picked_zmoco_relu_p_kernel(
             return raw
 
         x_bytes = turns.tile([P, T], U8, name="x_bytes", align_bytes=64, offset=0)
-        nc.gpsimd.memset(x_bytes[:].bitcast(I32), 0)
+        nc.vector.memset(x_bytes[:].bitcast(I32), 0)
         v_bytes = turns.tile([P, G], U8, name="v_bytes", align_bytes=64, offset=T)
         nc.vector.memset(v_bytes[:].bitcast(I32), 0)
 
         offs_sb = lists.tile([P, S // 16], U16, name="offs_sb")
         nc.sync.dma_start(offs_sb[:], offs)
-        x_table0 = sb.tile([P, T], I32, name="x_table0", tag="table", align_bytes=64)
-        nc.sync.dma_start(x_table0[:], words_of(x_words, 0))
+        x_table = [sb.tile([P, T], I32, name=f"x_table{o}", align_bytes=64) for o in range(2)]
+        nc.sync.dma_start(x_table[0][:], words_of(x_words, 0))
+        for q in range(QUADS):
+            nc.sync.dma_start(
+                x_bytes[32 * q : 32 * q + 8, :].bitcast(I32), x_scales[:, 4 * q : 4 * q + 4, :].bitcast(I32)
+            )
         neg_sb = lists.tile([P, V // 16], U16, name="neg_sb")
         nc.sync.dma_start(neg_sb[:], neg)
-        w_raw = [load_w(0), load_w(1)]
-        x_table1 = sb.tile([P, T], I32, name="x_table1", align_bytes=64)
-        nc.sync.dma_start(x_table1[:], words_of(x_words, 1))
-
+        w_raw = [load_w(0)]
         for q in range(QUADS):
-            nc.scalar.dma_start(
+            nc.sync.dma_start(
                 v_bytes[32 * q + V_PLANE : 32 * q + V_PLANE + 4, :].bitcast(I32),
                 v_scales[0, 4 * q : 4 * q + 4, :].bitcast(I32),
             )
-        for q in range(QUADS):
-            (nc.gpsimd if q < 3 else nc.scalar).dma_start(
-                x_bytes[32 * q : 32 * q + 8, :].bitcast(I32), x_scales[:, 4 * q : 4 * q + 4, :].bitcast(I32)
-            )
+        w_raw.append(load_w(1))
+        nc.sync.dma_start(x_table[1][:], words_of(x_words, 1))
+        v_table = turns.tile([P, G], I32, name="v_table", align_bytes=64, offset=4096)
+        nc.sync.dma_start(v_table[:], words_of(v_words, 0))
 
         x_codes = [sb.tile([P, S], U32, name=f"x_codes{o}", align_bytes=64) for o in range(2)]
         x_scale = sb.tile([P, S], U8, name="x_scale", align_bytes=64)
         v_codes = sb.tile([P, V], U32, name="v_codes", align_bytes=64)
         v_scale = sb.tile([P, V], U8, name="v_scale", align_bytes=64)
-        nc.vector.tensor_copy(x_codes[0][:], x_table0[:].bitcast(U32).indirect(offs_sb[:]))
-        v_table = sb.tile([P, G], I32, name="v_table", tag="table", align_bytes=64)
-        nc.sync.dma_start(v_table[:], words_of(v_words, 0))
-        nc.vector.tensor_copy(v_scale[:], v_bytes[:].indirect(neg_sb[:]))
+        nc.vector.tensor_copy(x_codes[0][:], x_table[0][:].bitcast(U32).indirect(offs_sb[:]))
         nc.vector.tensor_copy(x_scale[:], x_bytes[:].indirect(offs_sb[:]))
 
         w_bf = [
@@ -98,15 +96,31 @@ def tile_picked_zmoco_relu_p_kernel(
         def gather_x1(c):
             nc.vector.tensor_copy(
                 x_codes[1][:, CHUNK * c : CHUNK * (c + 1)],
-                x_table1[:].bitcast(U32).indirect(offs_sb[:, LIST_COLS * c : LIST_COLS * (c + 1)]),
+                x_table[1][:].bitcast(U32).indirect(offs_sb[:, LIST_COLS * c : LIST_COLS * (c + 1)]),
             )
 
-        nc.scalar.activation(dst[0], src[0], ACT.Copy)
-        nc.vector.tensor_copy(dst[1][:, :VECTOR_SHARE], src[1][:, :VECTOR_SHARE])
-        nc.scalar.activation(dst[1][:, VECTOR_SHARE:], src[1][:, VECTOR_SHARE:], ACT.Copy)
+        def cast_w(o):
+            cut = VECTOR_SHARE[o]
+            nc.vector.tensor_copy(dst[o][:, :cut], src[o][:, :cut])
+            nc.scalar.activation(dst[o][:, cut:], src[o][:, cut:], ACT.Copy)
+
+        cast_w(0)
+        nc.vector.tensor_copy(v_scale[:], v_bytes[:].indirect(neg_sb[:]))
         quantize_w(0, 0, PACK)
-        gather_x1(0)
+        y_acc = [psum.tile([P, V], F32, name=f"y_acc{c}") for c in range(CHUNKS)]
+        for c in range(1, CHUNKS):
+            nc.tensor.matmul_mx(
+                out=y_acc[c][:],
+                lhsT=w_codes[0][:, :P].bitcast(FP8X4),
+                lhsT_scale=w_scale[0][:, :P],
+                rhs=x_codes[0][:].bitcast(FP8X4),
+                rhs_scale=x_scale[:],
+                start=True,
+                stop=True,
+            )
+        cast_w(1)
         quantize_w(1, 0, 2)
+        gather_x1(0)
         quantize_w(1, 2, 4)
         for c in range(1, CHUNKS):
             gather_x1(c)
@@ -129,7 +143,10 @@ def tile_picked_zmoco_relu_p_kernel(
             h_bf.append(sb.tile([P, CHUNK, PACK], BF16, name=f"h_bf{c}", align_bytes=64))
             nc.scalar.activation(h_bf[c][:], h_acc[:].rearrange("p j t -> p t j"), ACT.Relu)
 
-        h_codes = [sb.tile([P, CHUNK], U32, name=f"h_codes{c}", align_bytes=64) for c in range(CHUNKS)]
+        h_codes = [
+            turns.tile([P, CHUNK], U32, name=f"h_codes{c}", align_bytes=64, offset=4096 + 4 * CHUNK * c)
+            for c in range(CHUNKS)
+        ]
         h_scale = [sb.tile([P, CHUNK], U8, name=f"h_scale{c}", align_bytes=64) for c in range(CHUNKS)]
 
         def quantize_h(c):
@@ -145,10 +162,10 @@ def tile_picked_zmoco_relu_p_kernel(
 
         e = [sb.tile([P, V], F32, name=f"e{c}") for c in range(CHUNKS)]
         total = [sb.tile([P, 1], F32, name=f"total{c}") for c in range(CHUNKS)]
-        for c in range(CHUNKS):
-            y_acc = psum.tile([P, V], F32, name=f"y_acc{c}")
+
+        def exponentials(c):
             nc.tensor.matmul_mx(
-                out=y_acc[:],
+                out=y_acc[c][:],
                 lhsT=h_codes[c][:].bitcast(FP8X4),
                 lhsT_scale=h_scale[c][:],
                 rhs=v_codes[:].bitcast(FP8X4),
@@ -157,12 +174,21 @@ def tile_picked_zmoco_relu_p_kernel(
                 stop=True,
             )
             neg_max = sb.tile([P, 1], F32, name=f"neg_max{c}")
-            nc.vector.tensor_reduce(neg_max[:], y_acc[:], mybir.AxisListType.X, ALU.max, negate=True)
-            nc.scalar.activation(e[c][:], y_acc[:], ACT.Exp, bias=neg_max[:], scale=1.0, accum_out=total[c][:])
+            nc.vector.tensor_reduce(neg_max[:], y_acc[c][:], mybir.AxisListType.X, ALU.max, negate=True)
+            nc.scalar.activation(e[c][:], y_acc[c][:], ACT.Exp, bias=neg_max[:], scale=1.0, accum_out=total[c][:])
 
-        for c in range(CHUNKS):
+        def normalise(c):
             inv = sb.tile([P, 1], F32, name=f"inv{c}")
             nc.vector.reciprocal(inv[:], total[c][:])
             prob = sb.tile([P, V], F32, name=f"prob{c}")
-            nc.vector.tensor_scalar(prob[:], e[c][:], inv[:], None, ALU.mult)
+            if c == 0:
+                nc.gpsimd.tensor_scalar(prob[:], e[c][:], inv[:], 0.0, ALU.mult, ALU.add)
+            else:
+                nc.vector.tensor_scalar(prob[:], e[c][:], inv[:], None, ALU.mult)
             nc.sync.dma_start(out[CHUNK * c : CHUNK * (c + 1), :], prob[:])
+
+        exponentials(0)
+        for c in range(1, CHUNKS):
+            exponentials(c)
+            normalise(c - 1)
+        normalise(CHUNKS - 1)

@@ -21,8 +21,8 @@ QUADS = 4
 CHUNK = 128
 CHUNKS = S // CHUNK
 LIST_COLS = CHUNK // 16
-VECTOR_SHARE = (48, 88)
-V_PLANE = 8
+VECTOR_SHARE = (32, 84)
+GPSIMD_CHUNKS = 1
 
 
 def tile_picked_zmoco_relu_p_kernel(
@@ -43,42 +43,46 @@ def tile_picked_zmoco_relu_p_kernel(
             nc.sync.dma_start(raw[:], w1[512 * o : 512 * (o + 1), :].rearrange("(p r) i -> p r i", r=PACK))
             return raw
 
-        x_bytes = turns.tile([P, T], U8, name="x_bytes", align_bytes=64, offset=0)
+        x_bytes = sb.tile([P, T], U8, name="x_bytes", align_bytes=64)
         nc.vector.memset(x_bytes[:].bitcast(I32), 0)
-        v_bytes = turns.tile([P, G], U8, name="v_bytes", align_bytes=64, offset=T)
-        nc.vector.memset(v_bytes[:].bitcast(I32), 0)
+        v_bytes = sb.tile([P, G], U8, name="v_bytes", align_bytes=64)
+        nc.gpsimd.memset(v_bytes[:].bitcast(I32), 0)
+        v_scale = sb.tile([P, V], U8, name="v_scale", align_bytes=64)
+        nc.gpsimd.memset(v_scale[:].bitcast(I32), 0)
+        minus_one = sb.tile([P, 1], F32, name="minus_one")
+        nc.gpsimd.memset(minus_one[:], -1.0)
 
-        offs_sb = lists.tile([P, S // 16], U16, name="offs_sb")
-        nc.sync.dma_start(offs_sb[:], offs)
         x_table = [sb.tile([P, T], I32, name=f"x_table{o}", align_bytes=64) for o in range(2)]
         nc.sync.dma_start(x_table[0][:], words_of(x_words, 0))
+        offs_sb = lists.tile([P, S // 16], U16, name="offs_sb")
+        nc.sync.dma_start(offs_sb[:], offs)
         for q in range(QUADS):
             nc.sync.dma_start(
                 x_bytes[32 * q : 32 * q + 8, :].bitcast(I32), x_scales[:, 4 * q : 4 * q + 4, :].bitcast(I32)
             )
+        w_raw = [load_w(0)]
+        nc.sync.dma_start(v_bytes[0:P:8, :].bitcast(I32), v_scales[0].bitcast(I32))
         neg_sb = lists.tile([P, V // 16], U16, name="neg_sb")
         nc.sync.dma_start(neg_sb[:], neg)
-        w_raw = [load_w(0)]
-        for q in range(QUADS):
-            nc.sync.dma_start(
-                v_bytes[32 * q + V_PLANE : 32 * q + V_PLANE + 4, :].bitcast(I32),
-                v_scales[0, 4 * q : 4 * q + 4, :].bitcast(I32),
-            )
         w_raw.append(load_w(1))
         nc.sync.dma_start(x_table[1][:], words_of(x_words, 1))
-        v_table = turns.tile([P, G], I32, name="v_table", align_bytes=64, offset=4096)
+        v_table = turns.tile([P, G], I32, name="v_table", align_bytes=64, offset=0)
         nc.sync.dma_start(v_table[:], words_of(v_words, 0))
 
-        x_codes = [sb.tile([P, S], U32, name=f"x_codes{o}", align_bytes=64) for o in range(2)]
+        spare = 4 * G
+        x0_codes = sb.tile([P, S], U32, name="x0_codes", align_bytes=64)
+        x1_first = sb.tile([P, CHUNK], U32, name="x1_first", align_bytes=64)
+        x1_rest = turns.tile([P, S - CHUNK], U32, name="x1_rest", align_bytes=64, offset=spare)
+        x_codes = [
+            [x0_codes[:, CHUNK * c : CHUNK * (c + 1)] for c in range(CHUNKS)],
+            [x1_first[:]] + [x1_rest[:, CHUNK * c : CHUNK * (c + 1)] for c in range(CHUNKS - 1)],
+        ]
         x_scale = sb.tile([P, S], U8, name="x_scale", align_bytes=64)
-        v_codes = sb.tile([P, V], U32, name="v_codes", align_bytes=64)
-        v_scale = sb.tile([P, V], U8, name="v_scale", align_bytes=64)
-        nc.vector.tensor_copy(x_codes[0][:], x_table[0][:].bitcast(U32).indirect(offs_sb[:]))
-        nc.vector.tensor_copy(x_scale[:], x_bytes[:].indirect(offs_sb[:]))
+        v_rows = turns.tile([P, V], U8, name="v_rows", align_bytes=64, offset=2 * spare)
 
         w_bf = [
             sb.tile([P, PACK, P, PACK], BF16, name="w_bf0", align_bytes=64),
-            turns.tile([P, PACK, P, PACK], BF16, name="w_bf1", align_bytes=64, offset=0),
+            turns.tile([P, PACK, P, PACK], BF16, name="w_bf1", align_bytes=64, offset=spare),
         ]
         w_codes = [sb.tile([P, H], U32, name=f"w_codes{o}", align_bytes=64) for o in range(2)]
         w_scale = [sb.tile([P, H], U8, name=f"w_scale{o}", align_bytes=64) for o in range(2)]
@@ -93,59 +97,77 @@ def tile_picked_zmoco_relu_p_kernel(
                 in_=w_bf[o][:, j0:j1].rearrange("p j m r -> p (j m r)"),
             )
 
-        def gather_x1(c):
-            nc.vector.tensor_copy(
-                x_codes[1][:, CHUNK * c : CHUNK * (c + 1)],
-                x_table[1][:].bitcast(U32).indirect(offs_sb[:, LIST_COLS * c : LIST_COLS * (c + 1)]),
-            )
-
         def cast_w(o):
             cut = VECTOR_SHARE[o]
             nc.vector.tensor_copy(dst[o][:, :cut], src[o][:, :cut])
             nc.scalar.activation(dst[o][:, cut:], src[o][:, cut:], ACT.Copy)
 
+        def gather_x(o, codes, c0, c1):
+            nc.vector.tensor_copy(
+                codes,
+                x_table[o][:].bitcast(U32).indirect(offs_sb[:, LIST_COLS * c0 : LIST_COLS * c1]),
+            )
+
+        gather_x(0, x0_codes[:], 0, CHUNKS)
+        nc.vector.tensor_copy(x_scale[:], x_bytes[:].indirect(offs_sb[:]))
         cast_w(0)
-        nc.vector.tensor_copy(v_scale[:], v_bytes[:].indirect(neg_sb[:]))
+        nc.vector.tensor_copy(v_rows[:], v_bytes[:].indirect(neg_sb[:]))
+        for q in range(QUADS):
+            nc.sync.dma_start(
+                v_scale[32 * q : 32 * q + 4, :].bitcast(I32), v_rows[32 * q : 32 * (q + 1) : 8, :].bitcast(I32)
+            )
         quantize_w(0, 0, PACK)
+
         y_acc = [psum.tile([P, V], F32, name=f"y_acc{c}") for c in range(CHUNKS)]
-        for c in range(1, CHUNKS):
+        for c, plane in ((1, x_scale), (2, x_scale), (3, v_rows)):
             nc.tensor.matmul_mx(
                 out=y_acc[c][:],
-                lhsT=w_codes[0][:, :P].bitcast(FP8X4),
-                lhsT_scale=w_scale[0][:, :P],
-                rhs=x_codes[0][:].bitcast(FP8X4),
-                rhs_scale=x_scale[:],
+                lhsT=x0_codes[:, :P].bitcast(FP8X4),
+                lhsT_scale=x_scale[:, :P],
+                rhs=x0_codes[:].bitcast(FP8X4),
+                rhs_scale=plane[:],
                 start=True,
                 stop=True,
             )
-        cast_w(1)
-        quantize_w(1, 0, 2)
-        gather_x1(0)
-        quantize_w(1, 2, 4)
-        for c in range(1, CHUNKS):
-            gather_x1(c)
+        h_acc = [psum.tile([P, PACK, CHUNK], F32, name=f"h_acc{c}") for c in range(CHUNKS)]
 
-        h_bf = []
+        def hidden_pass(c, j, o):
+            nc.tensor.matmul_mx(
+                out=h_acc[c][:, j, :],
+                lhsT=w_codes[o][:, P * j : P * (j + 1)].bitcast(FP8X4),
+                lhsT_scale=w_scale[o][:, P * j : P * (j + 1)],
+                rhs=x_codes[o][c].bitcast(FP8X4),
+                rhs_scale=x_scale[4 * o :, CHUNK * c : CHUNK * (c + 1)],
+                start=(o == 0),
+                stop=(o == 1),
+            )
+
         for c in range(CHUNKS):
-            cols = slice(CHUNK * c, CHUNK * (c + 1))
-            h_acc = psum.tile([P, PACK, CHUNK], F32, name=f"h_acc{c}")
-            for j in range(PACK):
+            hidden_pass(c, 0, 0)
+        cast_w(1)
+        gather_x(1, x_codes[1][0], 0, 1)
+        quantize_w(1, 0, 2)
+        quantize_w(1, 2, 4)
+        gather_x(1, x_codes[1][1], 1, 2)
+        gather_x(1, x1_rest[:, CHUNK:], 2, 4)
+
+        h_bf = [turns.tile([P, CHUNK, PACK], BF16, name="h_bf0", align_bytes=64, offset=3 * spare)] + [
+            sb.tile([P, CHUNK, PACK], BF16, name=f"h_bf{c}", align_bytes=64) for c in range(1, CHUNKS)
+        ]
+
+        def hidden(c):
+            hidden_pass(c, 0, 1)
+            for j in range(1, PACK):
                 for o in range(2):
-                    nc.tensor.matmul_mx(
-                        out=h_acc[:, j, :],
-                        lhsT=w_codes[o][:, P * j : P * (j + 1)].bitcast(FP8X4),
-                        lhsT_scale=w_scale[o][:, P * j : P * (j + 1)],
-                        rhs=x_codes[o][:, cols].bitcast(FP8X4),
-                        rhs_scale=x_scale[4 * o :, cols],
-                        start=(o == 0),
-                        stop=(o == 1),
-                    )
-            h_bf.append(sb.tile([P, CHUNK, PACK], BF16, name=f"h_bf{c}", align_bytes=64))
-            nc.scalar.activation(h_bf[c][:], h_acc[:].rearrange("p j t -> p t j"), ACT.Relu)
+                    hidden_pass(c, j, o)
+            nc.scalar.activation(h_bf[c][:], h_acc[c][:].rearrange("p j t -> p t j"), ACT.Relu)
+
+        for c in range(CHUNKS):
+            hidden(c)
 
         h_codes = [
-            turns.tile([P, CHUNK], U32, name=f"h_codes{c}", align_bytes=64, offset=4096 + 4 * CHUNK * c)
-            for c in range(CHUNKS)
+            turns.tile([P, CHUNK], U32, name=f"h_codes{c}", align_bytes=64, offset=where)
+            for c, where in enumerate((2 * spare, 0, 4 * CHUNK, 2 * spare))
         ]
         h_scale = [sb.tile([P, CHUNK], U8, name=f"h_scale{c}", align_bytes=64) for c in range(CHUNKS)]
 
@@ -156,39 +178,56 @@ def tile_picked_zmoco_relu_p_kernel(
                 in_=h_bf[c][:].rearrange("p t j -> p (t j)"),
             )
 
-        nc.vector.tensor_copy(v_codes[:], v_table[:].bitcast(U32).indirect(neg_sb[:]))
-        for c in range(CHUNKS):
+        v_codes = [
+            sb.tile([P, V // 2], U32, name="v_codes0", align_bytes=64),
+            turns.tile([P, V // 2], U32, name="v_codes1", align_bytes=64, offset=3 * spare),
+        ]
+
+        def gather_v(half):
+            nc.vector.tensor_copy(
+                v_codes[half][:],
+                v_table[:].bitcast(U32).indirect(neg_sb[:, V // 32 * half : V // 32 * (half + 1)]),
+            )
+
+        gather_v(0)
+        quantize_h(0)
+        gather_v(1)
+        for c in range(1, CHUNKS - 1):
             quantize_h(c)
 
         e = [sb.tile([P, V], F32, name=f"e{c}") for c in range(CHUNKS)]
         total = [sb.tile([P, 1], F32, name=f"total{c}") for c in range(CHUNKS)]
 
         def exponentials(c):
-            nc.tensor.matmul_mx(
-                out=y_acc[c][:],
-                lhsT=h_codes[c][:].bitcast(FP8X4),
-                lhsT_scale=h_scale[c][:],
-                rhs=v_codes[:].bitcast(FP8X4),
-                rhs_scale=v_scale[V_PLANE:, :],
-                start=True,
-                stop=True,
-            )
+            for half in range(2):
+                cols = slice(V // 2 * half, V // 2 * (half + 1))
+                nc.tensor.matmul_mx(
+                    out=y_acc[c][:, cols],
+                    lhsT=h_codes[c][:].bitcast(FP8X4),
+                    lhsT_scale=h_scale[c][:],
+                    rhs=v_codes[half][:].bitcast(FP8X4),
+                    rhs_scale=v_scale[:, cols],
+                    start=True,
+                    stop=True,
+                )
             neg_max = sb.tile([P, 1], F32, name=f"neg_max{c}")
             nc.vector.tensor_reduce(neg_max[:], y_acc[c][:], mybir.AxisListType.X, ALU.max, negate=True)
             nc.scalar.activation(e[c][:], y_acc[c][:], ACT.Exp, bias=neg_max[:], scale=1.0, accum_out=total[c][:])
 
         def normalise(c):
             inv = sb.tile([P, 1], F32, name=f"inv{c}")
-            nc.vector.reciprocal(inv[:], total[c][:])
             prob = sb.tile([P, V], F32, name=f"prob{c}")
-            if c == 0:
+            if c < GPSIMD_CHUNKS:
+                nc.gpsimd.tensor_tensor(inv[:], total[c][:], minus_one[:], ALU.pow)
                 nc.gpsimd.tensor_scalar(prob[:], e[c][:], inv[:], 0.0, ALU.mult, ALU.add)
             else:
+                nc.vector.reciprocal(inv[:], total[c][:])
                 nc.vector.tensor_scalar(prob[:], e[c][:], inv[:], None, ALU.mult)
             nc.sync.dma_start(out[CHUNK * c : CHUNK * (c + 1), :], prob[:])
 
         exponentials(0)
+        quantize_h(CHUNKS - 1)
         for c in range(1, CHUNKS):
             exponentials(c)
-            normalise(c - 1)
-        normalise(CHUNKS - 1)
+        for c in range(CHUNKS):
+            normalise(c)

@@ -43,14 +43,14 @@ def tile_picked_zmoco_relu_p_kernel(
             nc.sync.dma_start(raw[:], w1[512 * o : 512 * (o + 1), :].rearrange("(p r) i -> p r i", r=PACK))
             return raw
 
-        x_bytes = sb.tile([P, T], U8, name="x_bytes", align_bytes=64)
+        x_bytes = turns.tile([P, T], U8, name="x_bytes", align_bytes=64, offset=0)
         nc.vector.memset(x_bytes[:].bitcast(I32), 0)
+        x1_scale = sb.tile([P, S], U8, name="x1_scale", align_bytes=64)
+        nc.vector.memset(x1_scale[:].bitcast(I32), 0)
         v_bytes = sb.tile([P, G], U8, name="v_bytes", align_bytes=64)
         nc.gpsimd.memset(v_bytes[:].bitcast(I32), 0)
         v_scale = sb.tile([P, V], U8, name="v_scale", align_bytes=64)
         nc.gpsimd.memset(v_scale[:].bitcast(I32), 0)
-        minus_one = sb.tile([P, 1], F32, name="minus_one")
-        nc.gpsimd.memset(minus_one[:], -1.0)
 
         x_table = [sb.tile([P, T], I32, name=f"x_table{o}", align_bytes=64) for o in range(2)]
         nc.sync.dma_start(x_table[0][:], words_of(x_words, 0))
@@ -58,16 +58,15 @@ def tile_picked_zmoco_relu_p_kernel(
         nc.sync.dma_start(offs_sb[:], offs)
         for q in range(QUADS):
             nc.sync.dma_start(
-                x_bytes[32 * q : 32 * q + 8, :].bitcast(I32), x_scales[:, 4 * q : 4 * q + 4, :].bitcast(I32)
+                x_bytes[32 * q : 32 * q + 4, :].bitcast(I32), x_scales[0, 4 * q : 4 * q + 4, :].bitcast(I32)
             )
+        nc.scalar.dma_start(x_bytes[4:P:8, :].bitcast(I32), x_scales[1].bitcast(I32))
         w_raw = [load_w(0)]
         nc.sync.dma_start(v_bytes[0:P:8, :].bitcast(I32), v_scales[0].bitcast(I32))
         neg_sb = lists.tile([P, V // 16], U16, name="neg_sb")
         nc.sync.dma_start(neg_sb[:], neg)
         w_raw.append(load_w(1))
         nc.sync.dma_start(x_table[1][:], words_of(x_words, 1))
-        v_table = turns.tile([P, G], I32, name="v_table", align_bytes=64, offset=0)
-        nc.sync.dma_start(v_table[:], words_of(v_words, 0))
 
         spare = 4 * G
         x0_codes = sb.tile([P, S], U32, name="x0_codes", align_bytes=64)
@@ -78,7 +77,7 @@ def tile_picked_zmoco_relu_p_kernel(
             [x1_first[:]] + [x1_rest[:, CHUNK * c : CHUNK * (c + 1)] for c in range(CHUNKS - 1)],
         ]
         x_scale = sb.tile([P, S], U8, name="x_scale", align_bytes=64)
-        v_rows = turns.tile([P, V], U8, name="v_rows", align_bytes=64, offset=2 * spare)
+        v_rows = sb.tile([P, V], U8, name="v_rows", align_bytes=64)
 
         w_bf = [
             sb.tile([P, PACK, P, PACK], BF16, name="w_bf0", align_bytes=64),
@@ -110,6 +109,12 @@ def tile_picked_zmoco_relu_p_kernel(
 
         gather_x(0, x0_codes[:], 0, CHUNKS)
         nc.vector.tensor_copy(x_scale[:], x_bytes[:].indirect(offs_sb[:]))
+        for q in range(QUADS):
+            nc.sync.dma_start(
+                x1_scale[32 * q : 32 * q + 4, :].bitcast(I32), x_scale[32 * q + 4 : 32 * (q + 1) : 8, :].bitcast(I32)
+            )
+        v_table = turns.tile([P, G], I32, name="v_table", align_bytes=64, offset=0)
+        nc.sync.dma_start(v_table[:], words_of(v_words, 0))
         cast_w(0)
         nc.vector.tensor_copy(v_rows[:], v_bytes[:].indirect(neg_sb[:]))
         for q in range(QUADS):
@@ -137,7 +142,7 @@ def tile_picked_zmoco_relu_p_kernel(
                 lhsT=w_codes[o][:, P * j : P * (j + 1)].bitcast(FP8X4),
                 lhsT_scale=w_scale[o][:, P * j : P * (j + 1)],
                 rhs=x_codes[o][c].bitcast(FP8X4),
-                rhs_scale=x_scale[4 * o :, CHUNK * c : CHUNK * (c + 1)],
+                rhs_scale=(x_scale, x1_scale)[o][:, CHUNK * c : CHUNK * (c + 1)],
                 start=(o == 0),
                 stop=(o == 1),
             )
@@ -151,9 +156,7 @@ def tile_picked_zmoco_relu_p_kernel(
         gather_x(1, x_codes[1][1], 1, 2)
         gather_x(1, x1_rest[:, CHUNK:], 2, 4)
 
-        h_bf = [turns.tile([P, CHUNK, PACK], BF16, name="h_bf0", align_bytes=64, offset=3 * spare)] + [
-            sb.tile([P, CHUNK, PACK], BF16, name=f"h_bf{c}", align_bytes=64) for c in range(1, CHUNKS)
-        ]
+        h_bf = [sb.tile([P, CHUNK, PACK], BF16, name=f"h_bf{c}", align_bytes=64) for c in range(CHUNKS)]
 
         def hidden(c):
             hidden_pass(c, 0, 1)
@@ -178,10 +181,7 @@ def tile_picked_zmoco_relu_p_kernel(
                 in_=h_bf[c][:].rearrange("p t j -> p (t j)"),
             )
 
-        v_codes = [
-            sb.tile([P, V // 2], U32, name="v_codes0", align_bytes=64),
-            turns.tile([P, V // 2], U32, name="v_codes1", align_bytes=64, offset=3 * spare),
-        ]
+        v_codes = [sb.tile([P, V // 2], U32, name=f"v_codes{half}", align_bytes=64) for half in range(2)]
 
         def gather_v(half):
             nc.vector.tensor_copy(
@@ -189,8 +189,8 @@ def tile_picked_zmoco_relu_p_kernel(
                 v_table[:].bitcast(U32).indirect(neg_sb[:, V // 32 * half : V // 32 * (half + 1)]),
             )
 
-        gather_v(0)
         quantize_h(0)
+        gather_v(0)
         gather_v(1)
         for c in range(1, CHUNKS - 1):
             quantize_h(c)
@@ -214,20 +214,22 @@ def tile_picked_zmoco_relu_p_kernel(
             nc.vector.tensor_reduce(neg_max[:], y_acc[c][:], mybir.AxisListType.X, ALU.max, negate=True)
             nc.scalar.activation(e[c][:], y_acc[c][:], ACT.Exp, bias=neg_max[:], scale=1.0, accum_out=total[c][:])
 
+        inv = [sb.tile([P, 1], F32, name=f"inv{c}") for c in range(CHUNKS)]
+
         def normalise(c):
-            inv = sb.tile([P, 1], F32, name=f"inv{c}")
             prob = sb.tile([P, V], F32, name=f"prob{c}")
             if c < GPSIMD_CHUNKS:
-                nc.gpsimd.tensor_tensor(inv[:], total[c][:], minus_one[:], ALU.pow)
-                nc.gpsimd.tensor_scalar(prob[:], e[c][:], inv[:], 0.0, ALU.mult, ALU.add)
+                nc.gpsimd.tensor_scalar(prob[:], e[c][:], inv[c][:], 0.0, ALU.mult, ALU.add)
             else:
-                nc.vector.reciprocal(inv[:], total[c][:])
-                nc.vector.tensor_scalar(prob[:], e[c][:], inv[:], None, ALU.mult)
+                nc.vector.tensor_scalar(prob[:], e[c][:], inv[c][:], None, ALU.mult)
             nc.sync.dma_start(out[CHUNK * c : CHUNK * (c + 1), :], prob[:])
 
         exponentials(0)
         quantize_h(CHUNKS - 1)
         for c in range(1, CHUNKS):
             exponentials(c)
-        for c in range(CHUNKS):
+            nc.vector.reciprocal(inv[c - 1][:], total[c - 1][:])
+        for c in range(CHUNKS - 1):
             normalise(c)
+        nc.vector.reciprocal(inv[CHUNKS - 1][:], total[CHUNKS - 1][:])
+        normalise(CHUNKS - 1)

@@ -124,16 +124,6 @@ def tile_picked_zmoco_relu_p_kernel(
         quantize_w(0, 0, PACK)
 
         y_acc = [psum.tile([P, V], F32, name=f"y_acc{c}") for c in range(CHUNKS)]
-        for c, plane in ((1, x_scale), (2, x_scale), (3, v_rows)):
-            nc.tensor.matmul_mx(
-                out=y_acc[c][:],
-                lhsT=x0_codes[:, :P].bitcast(FP8X4),
-                lhsT_scale=x_scale[:, :P],
-                rhs=x0_codes[:].bitcast(FP8X4),
-                rhs_scale=plane[:],
-                start=True,
-                stop=True,
-            )
         h_acc = [psum.tile([P, PACK, CHUNK], F32, name=f"h_acc{c}") for c in range(CHUNKS)]
 
         def hidden_pass(c, j, o):

@@ -43,10 +43,8 @@ def tile_picked_zmoco_relu_p_kernel(
             nc.sync.dma_start(raw[:], w1[512 * o : 512 * (o + 1), :].rearrange("(p r) i -> p r i", r=PACK))
             return raw
 
-        x_bytes = turns.tile([P, T], U8, name="x_bytes", align_bytes=64, offset=0)
+        x_bytes = sb.tile([P, T], U8, name="x_bytes", align_bytes=64)
         nc.vector.memset(x_bytes[:].bitcast(I32), 0)
-        x1_scale = sb.tile([P, S], U8, name="x1_scale", align_bytes=64)
-        nc.vector.memset(x1_scale[:].bitcast(I32), 0)
         v_bytes = sb.tile([P, G], U8, name="v_bytes", align_bytes=64)
         nc.gpsimd.memset(v_bytes[:].bitcast(I32), 0)
         v_scale = sb.tile([P, V], U8, name="v_scale", align_bytes=64)
@@ -58,15 +56,16 @@ def tile_picked_zmoco_relu_p_kernel(
         nc.sync.dma_start(offs_sb[:], offs)
         for q in range(QUADS):
             nc.sync.dma_start(
-                x_bytes[32 * q : 32 * q + 4, :].bitcast(I32), x_scales[0, 4 * q : 4 * q + 4, :].bitcast(I32)
+                x_bytes[32 * q : 32 * q + 8, :].bitcast(I32), x_scales[:, 4 * q : 4 * q + 4, :].bitcast(I32)
             )
-        nc.scalar.dma_start(x_bytes[4:P:8, :].bitcast(I32), x_scales[1].bitcast(I32))
         w_raw = [load_w(0)]
         nc.sync.dma_start(v_bytes[0:P:8, :].bitcast(I32), v_scales[0].bitcast(I32))
         neg_sb = lists.tile([P, V // 16], U16, name="neg_sb")
         nc.sync.dma_start(neg_sb[:], neg)
         w_raw.append(load_w(1))
         nc.sync.dma_start(x_table[1][:], words_of(x_words, 1))
+        v_table = turns.tile([P, G], I32, name="v_table", align_bytes=64, offset=0)
+        nc.sync.dma_start(v_table[:], words_of(v_words, 0))
 
         spare = 4 * G
         x0_codes = sb.tile([P, S], U32, name="x0_codes", align_bytes=64)
@@ -109,12 +108,6 @@ def tile_picked_zmoco_relu_p_kernel(
 
         gather_x(0, x0_codes[:], 0, CHUNKS)
         nc.vector.tensor_copy(x_scale[:], x_bytes[:].indirect(offs_sb[:]))
-        for q in range(QUADS):
-            nc.sync.dma_start(
-                x1_scale[32 * q : 32 * q + 4, :].bitcast(I32), x_scale[32 * q + 4 : 32 * (q + 1) : 8, :].bitcast(I32)
-            )
-        v_table = turns.tile([P, G], I32, name="v_table", align_bytes=64, offset=0)
-        nc.sync.dma_start(v_table[:], words_of(v_words, 0))
         cast_w(0)
         nc.vector.tensor_copy(v_rows[:], v_bytes[:].indirect(neg_sb[:]))
         for q in range(QUADS):
@@ -132,7 +125,7 @@ def tile_picked_zmoco_relu_p_kernel(
                 lhsT=w_codes[o][:, P * j : P * (j + 1)].bitcast(FP8X4),
                 lhsT_scale=w_scale[o][:, P * j : P * (j + 1)],
                 rhs=x_codes[o][c].bitcast(FP8X4),
-                rhs_scale=(x_scale, x1_scale)[o][:, CHUNK * c : CHUNK * (c + 1)],
+                rhs_scale=x_scale[4 * o :, CHUNK * c : CHUNK * (c + 1)],
                 start=(o == 0),
                 stop=(o == 1),
             )

@@ -20,8 +20,7 @@ PACK = 4
 QUADS = 4
 CHUNK = 128
 CHUNKS = S // CHUNK
-LIST_COLS = CHUNK // 16
-VECTOR_SHARE = (32, 84)
+VECTOR_SHARE = 84
 GPSIMD_CHUNKS = 1
 
 
@@ -62,26 +61,17 @@ def tile_picked_zmoco_relu_p_kernel(
         nc.sync.dma_start(v_bytes[0:P:8, :].bitcast(I32), v_scales[0].bitcast(I32))
         neg_sb = lists.tile([P, V // 16], U16, name="neg_sb")
         nc.sync.dma_start(neg_sb[:], neg)
-        w_raw.append(load_w(1))
         nc.sync.dma_start(x_table[1][:], words_of(x_words, 1))
+        w_raw.append(load_w(1))
         v_table = turns.tile([P, G], I32, name="v_table", align_bytes=64, offset=0)
         nc.sync.dma_start(v_table[:], words_of(v_words, 0))
 
         spare = 4 * G
-        x0_codes = sb.tile([P, S], U32, name="x0_codes", align_bytes=64)
-        x1_first = sb.tile([P, CHUNK], U32, name="x1_first", align_bytes=64)
-        x1_rest = turns.tile([P, S - CHUNK], U32, name="x1_rest", align_bytes=64, offset=spare)
-        x_codes = [
-            [x0_codes[:, CHUNK * c : CHUNK * (c + 1)] for c in range(CHUNKS)],
-            [x1_first[:]] + [x1_rest[:, CHUNK * c : CHUNK * (c + 1)] for c in range(CHUNKS - 1)],
-        ]
+        x_codes = [sb.tile([P, S], U32, name=f"x_codes{o}", align_bytes=64) for o in range(2)]
         x_scale = sb.tile([P, S], U8, name="x_scale", align_bytes=64)
         v_rows = sb.tile([P, V], U8, name="v_rows", align_bytes=64)
 
-        w_bf = [
-            sb.tile([P, PACK, P, PACK], BF16, name="w_bf0", align_bytes=64),
-            turns.tile([P, PACK, P, PACK], BF16, name="w_bf1", align_bytes=64, offset=spare),
-        ]
+        w_bf = [sb.tile([P, PACK, P, PACK], BF16, name=f"w_bf{o}", align_bytes=64) for o in range(2)]
         w_codes = [sb.tile([P, H], U32, name=f"w_codes{o}", align_bytes=64) for o in range(2)]
         w_scale = [sb.tile([P, H], U8, name=f"w_scale{o}", align_bytes=64) for o in range(2)]
         src = [w_raw[o][:].rearrange("p r (m j) -> p m r j", j=PACK) for o in range(2)]
@@ -95,25 +85,18 @@ def tile_picked_zmoco_relu_p_kernel(
                 in_=w_bf[o][:, j0:j1].rearrange("p j m r -> p (j m r)"),
             )
 
-        def cast_w(o):
-            cut = VECTOR_SHARE[o]
-            nc.vector.tensor_copy(dst[o][:, :cut], src[o][:, :cut])
-            nc.scalar.activation(dst[o][:, cut:], src[o][:, cut:], ACT.Copy)
+        def gather_x(o):
+            nc.vector.tensor_copy(x_codes[o][:], x_table[o][:].bitcast(U32).indirect(offs_sb[:]))
 
-        def gather_x(o, codes, c0, c1):
-            nc.vector.tensor_copy(
-                codes,
-                x_table[o][:].bitcast(U32).indirect(offs_sb[:, LIST_COLS * c0 : LIST_COLS * c1]),
-            )
-
-        gather_x(0, x0_codes[:], 0, CHUNKS)
+        gather_x(0)
         nc.vector.tensor_copy(x_scale[:], x_bytes[:].indirect(offs_sb[:]))
-        cast_w(0)
+        nc.scalar.activation(dst[0], src[0], ACT.Copy)
         nc.vector.tensor_copy(v_rows[:], v_bytes[:].indirect(neg_sb[:]))
         for q in range(QUADS):
             nc.sync.dma_start(
                 v_scale[32 * q : 32 * q + 4, :].bitcast(I32), v_rows[32 * q : 32 * (q + 1) : 8, :].bitcast(I32)
             )
+        gather_x(1)
         quantize_w(0, 0, PACK)
 
         y_acc = [psum.tile([P, V], F32, name=f"y_acc{c}") for c in range(CHUNKS)]
@@ -124,28 +107,25 @@ def tile_picked_zmoco_relu_p_kernel(
                 out=h_acc[c][:, j, :],
                 lhsT=w_codes[o][:, P * j : P * (j + 1)].bitcast(FP8X4),
                 lhsT_scale=w_scale[o][:, P * j : P * (j + 1)],
-                rhs=x_codes[o][c].bitcast(FP8X4),
+                rhs=x_codes[o][:, CHUNK * c : CHUNK * (c + 1)].bitcast(FP8X4),
                 rhs_scale=x_scale[4 * o :, CHUNK * c : CHUNK * (c + 1)],
-                start=(o == 0),
-                stop=(o == 1),
+                start=(o == 0 and j == 0),
+                stop=(o == 1 and j == PACK - 1),
             )
 
         for c in range(CHUNKS):
-            hidden_pass(c, 0, 0)
-        cast_w(1)
-        gather_x(1, x_codes[1][0], 0, 1)
+            for j in range(PACK):
+                hidden_pass(c, j, 0)
+        nc.vector.tensor_copy(dst[1][:, :VECTOR_SHARE], src[1][:, :VECTOR_SHARE])
+        nc.scalar.activation(dst[1][:, VECTOR_SHARE:], src[1][:, VECTOR_SHARE:], ACT.Copy)
         quantize_w(1, 0, 2)
         quantize_w(1, 2, 4)
-        gather_x(1, x_codes[1][1], 1, 2)
-        gather_x(1, x1_rest[:, CHUNK:], 2, 4)
 
         h_bf = [sb.tile([P, CHUNK, PACK], BF16, name=f"h_bf{c}", align_bytes=64) for c in range(CHUNKS)]
 
         def hidden(c):
-            hidden_pass(c, 0, 1)
-            for j in range(1, PACK):
-                for o in range(2):
-                    hidden_pass(c, j, o)
+            for j in range(PACK):
+                hidden_pass(c, j, 1)
             nc.scalar.activation(h_bf[c][:], h_acc[c][:].rearrange("p j t -> p t j"), ACT.Relu)
 
         for c in range(CHUNKS):
@@ -172,8 +152,8 @@ def tile_picked_zmoco_relu_p_kernel(
                 v_table[:].bitcast(U32).indirect(neg_sb[:, V // 32 * half : V // 32 * (half + 1)]),
             )
 
-        quantize_h(0)
         gather_v(0)
+        quantize_h(0)
         gather_v(1)
         for c in range(1, CHUNKS - 1):
             quantize_h(c)

@@ -20,7 +20,7 @@ PACK = 4
 QUADS = 4
 CHUNK = 128
 CHUNKS = S // CHUNK
-VECTOR_SHARE = 84
+LIST_COLS = CHUNK // 16
 GPSIMD_CHUNKS = 1
 
 
@@ -45,11 +45,13 @@ def tile_picked_zmoco_relu_p_kernel(
         x_bytes = sb.tile([P, T], U8, name="x_bytes", align_bytes=64)
         nc.vector.memset(x_bytes[:].bitcast(I32), 0)
         v_bytes = sb.tile([P, G], U8, name="v_bytes", align_bytes=64)
-        nc.gpsimd.memset(v_bytes[:].bitcast(I32), 0)
+        nc.vector.memset(v_bytes[:].bitcast(I32), 0)
         v_scale = sb.tile([P, V], U8, name="v_scale", align_bytes=64)
-        nc.gpsimd.memset(v_scale[:].bitcast(I32), 0)
+        nc.vector.memset(v_scale[:].bitcast(I32), 0)
 
         x_table = [sb.tile([P, T], I32, name=f"x_table{o}", align_bytes=64) for o in range(2)]
+        neg_sb = lists.tile([P, V // 16], U16, name="neg_sb")
+        nc.sync.dma_start(neg_sb[:], neg)
         nc.sync.dma_start(x_table[0][:], words_of(x_words, 0))
         offs_sb = lists.tile([P, S // 16], U16, name="offs_sb")
         nc.sync.dma_start(offs_sb[:], offs)
@@ -59,45 +61,62 @@ def tile_picked_zmoco_relu_p_kernel(
             )
         w_raw = [load_w(0)]
         nc.sync.dma_start(v_bytes[0:P:8, :].bitcast(I32), v_scales[0].bitcast(I32))
-        neg_sb = lists.tile([P, V // 16], U16, name="neg_sb")
-        nc.sync.dma_start(neg_sb[:], neg)
-        nc.sync.dma_start(x_table[1][:], words_of(x_words, 1))
         w_raw.append(load_w(1))
+        nc.sync.dma_start(x_table[1][:], words_of(x_words, 1))
         v_table = turns.tile([P, G], I32, name="v_table", align_bytes=64, offset=0)
         nc.sync.dma_start(v_table[:], words_of(v_words, 0))
 
         spare = 4 * G
-        x_codes = [sb.tile([P, S], U32, name=f"x_codes{o}", align_bytes=64) for o in range(2)]
+        x0_codes = sb.tile([P, S], U32, name="x0_codes", align_bytes=64)
+        x1_first = sb.tile([P, CHUNK], U32, name="x1_first", align_bytes=64)
+        x1_rest = turns.tile([P, S - CHUNK], U32, name="x1_rest", align_bytes=64, offset=spare + 12 * S)
+        x_codes = [
+            [x0_codes[:, CHUNK * c : CHUNK * (c + 1)] for c in range(CHUNKS)],
+            [x1_first[:]] + [x1_rest[:, CHUNK * c : CHUNK * (c + 1)] for c in range(CHUNKS - 1)],
+        ]
         x_scale = sb.tile([P, S], U8, name="x_scale", align_bytes=64)
-        v_rows = sb.tile([P, V], U8, name="v_rows", align_bytes=64)
+        late = spare + 16 * S
+        v_rows = turns.tile([P, V], U8, name="v_rows", align_bytes=64, offset=late + 8 * S)
 
-        w_bf = [sb.tile([P, PACK, P, PACK], BF16, name=f"w_bf{o}", align_bytes=64) for o in range(2)]
+        w_bf = [
+            [
+                turns.tile([P, 2, P, PACK], BF16, name=f"w_bf{o}{half}", align_bytes=64, offset=spare + 4 * S * (2 * o + half))
+                for half in range(2)
+            ]
+            for o in range(2)
+        ]
         w_codes = [sb.tile([P, H], U32, name=f"w_codes{o}", align_bytes=64) for o in range(2)]
         w_scale = [sb.tile([P, H], U8, name=f"w_scale{o}", align_bytes=64) for o in range(2)]
         src = [w_raw[o][:].rearrange("p r (m j) -> p m r j", j=PACK) for o in range(2)]
-        dst = [w_bf[o][:].rearrange("p j m r -> p m r j") for o in range(2)]
+        dst = [[w_bf[o][half][:].rearrange("p j m r -> p m r j") for half in range(2)] for o in range(2)]
 
-        def quantize_w(o, j0, j1):
-            cols = slice(P * j0, P * j1)
+        def quantize_w(o, half):
+            cols = slice(2 * P * half, 2 * P * (half + 1))
             nc.vector.quantize_mx(
                 out=w_codes[o][:, cols].bitcast(FP8X4),
                 scales=w_scale[o][:, cols],
-                in_=w_bf[o][:, j0:j1].rearrange("p j m r -> p (j m r)"),
+                in_=w_bf[o][half][:].rearrange("p j m r -> p (j m r)"),
             )
 
-        def gather_x(o):
-            nc.vector.tensor_copy(x_codes[o][:], x_table[o][:].bitcast(U32).indirect(offs_sb[:]))
+        def gather_x(o, codes, c0, c1):
+            nc.vector.tensor_copy(
+                codes,
+                x_table[o][:].bitcast(U32).indirect(offs_sb[:, LIST_COLS * c0 : LIST_COLS * c1]),
+            )
 
-        gather_x(0)
+        gather_x(0, x0_codes[:], 0, CHUNKS)
         nc.vector.tensor_copy(x_scale[:], x_bytes[:].indirect(offs_sb[:]))
-        nc.scalar.activation(dst[0], src[0], ACT.Copy)
+        for half in range(2):
+            nc.scalar.activation(dst[0][half], src[0][:, :, :, 2 * half : 2 * half + 2], ACT.Copy)
         nc.vector.tensor_copy(v_rows[:], v_bytes[:].indirect(neg_sb[:]))
         for q in range(QUADS):
             nc.sync.dma_start(
                 v_scale[32 * q : 32 * q + 4, :].bitcast(I32), v_rows[32 * q : 32 * (q + 1) : 8, :].bitcast(I32)
             )
-        gather_x(1)
-        quantize_w(0, 0, PACK)
+        quantize_w(0, 0)
+        nc.vector.tensor_copy(dst[1][0], src[1][:, :, :, :2])
+        nc.scalar.activation(dst[1][1], src[1][:, :, :, 2:], ACT.Copy)
+        quantize_w(0, 1)
 
         y_acc = [psum.tile([P, V], F32, name=f"y_acc{c}") for c in range(CHUNKS)]
         h_acc = [psum.tile([P, PACK, CHUNK], F32, name=f"h_acc{c}") for c in range(CHUNKS)]
@@ -107,21 +126,26 @@ def tile_picked_zmoco_relu_p_kernel(
                 out=h_acc[c][:, j, :],
                 lhsT=w_codes[o][:, P * j : P * (j + 1)].bitcast(FP8X4),
                 lhsT_scale=w_scale[o][:, P * j : P * (j + 1)],
-                rhs=x_codes[o][:, CHUNK * c : CHUNK * (c + 1)].bitcast(FP8X4),
+                rhs=x_codes[o][c].bitcast(FP8X4),
                 rhs_scale=x_scale[4 * o :, CHUNK * c : CHUNK * (c + 1)],
                 start=(o == 0 and j == 0),
                 stop=(o == 1 and j == PACK - 1),
             )
 
-        for c in range(CHUNKS):
-            for j in range(PACK):
-                hidden_pass(c, j, 0)
-        nc.vector.tensor_copy(dst[1][:, :VECTOR_SHARE], src[1][:, :VECTOR_SHARE])
-        nc.scalar.activation(dst[1][:, VECTOR_SHARE:], src[1][:, VECTOR_SHARE:], ACT.Copy)
-        quantize_w(1, 0, 2)
-        quantize_w(1, 2, 4)
+        for half in range(2):
+            for c in range(CHUNKS):
+                for j in range(2):
+                    hidden_pass(c, 2 * half + j, 0)
+        quantize_w(1, 0)
+        gather_x(1, x_codes[1][0], 0, 1)
+        quantize_w(1, 1)
+        gather_x(1, x_codes[1][1], 1, 2)
+        gather_x(1, x1_rest[:, CHUNK:], 2, 4)
 
-        h_bf = [sb.tile([P, CHUNK, PACK], BF16, name=f"h_bf{c}", align_bytes=64) for c in range(CHUNKS)]
+        h_bf = [
+            turns.tile([P, CHUNK, PACK], BF16, name=f"h_bf{c}", align_bytes=64, offset=late + 8 * CHUNK * c)
+            for c in range(CHUNKS)
+        ]
 
         def hidden(c):
             for j in range(PACK):
@@ -133,7 +157,7 @@ def tile_picked_zmoco_relu_p_kernel(
 
         h_codes = [
             turns.tile([P, CHUNK], U32, name=f"h_codes{c}", align_bytes=64, offset=where)
-            for c, where in enumerate((2 * spare, 0, 4 * CHUNK, 2 * spare))
+            for c, where in enumerate((late + 8 * S, 0, 4 * CHUNK, late + 8 * S))
         ]
         h_scale = [sb.tile([P, CHUNK], U8, name=f"h_scale{c}", align_bytes=64) for c in range(CHUNKS)]
 
@@ -144,7 +168,10 @@ def tile_picked_zmoco_relu_p_kernel(
                 in_=h_bf[c][:].rearrange("p t j -> p (t j)"),
             )
 
-        v_codes = [sb.tile([P, V // 2], U32, name=f"v_codes{half}", align_bytes=64) for half in range(2)]
+        v_codes = [
+            sb.tile([P, V // 2], U32, name="v_codes0", align_bytes=64),
+            turns.tile([P, V // 2], U32, name="v_codes1", align_bytes=64, offset=late),
+        ]
 
         def gather_v(half):
             nc.vector.tensor_copy(

@@ -22,6 +22,8 @@ CHUNK = 128
 CHUNKS = S // CHUNK
 LIST_COLS = CHUNK // 16
 GPSIMD_CHUNKS = 1
+ROWS_AHEAD = 3
+V_ROWS_AT = 8
 
 
 def tile_picked_zmoco_relu_p_kernel(
@@ -42,10 +44,10 @@ def tile_picked_zmoco_relu_p_kernel(
             nc.sync.dma_start(raw[:], w1[512 * o : 512 * (o + 1), :].rearrange("(p r) i -> p r i", r=PACK))
             return raw
 
-        x_bytes = sb.tile([P, T], U8, name="x_bytes", align_bytes=64)
-        nc.vector.memset(x_bytes[:].bitcast(I32), 0)
         v_bytes = sb.tile([P, G], U8, name="v_bytes", align_bytes=64)
         nc.vector.memset(v_bytes[:].bitcast(I32), 0)
+        x_bytes = sb.tile([P, T], U8, name="x_bytes", align_bytes=64)
+        nc.vector.memset(x_bytes[:].bitcast(I32), 0)
         v_scale = sb.tile([P, V], U8, name="v_scale", align_bytes=64)
         nc.vector.memset(v_scale[:].bitcast(I32), 0)
 
@@ -55,12 +57,17 @@ def tile_picked_zmoco_relu_p_kernel(
         nc.sync.dma_start(x_table[0][:], words_of(x_words, 0))
         offs_sb = lists.tile([P, S // 16], U16, name="offs_sb")
         nc.sync.dma_start(offs_sb[:], offs)
-        for q in range(QUADS):
-            nc.sync.dma_start(
-                x_bytes[32 * q : 32 * q + 8, :].bitcast(I32), x_scales[:, 4 * q : 4 * q + 4, :].bitcast(I32)
-            )
+        nc.sync.dma_start(v_bytes[V_ROWS_AT : V_ROWS_AT + 16, :].bitcast(I32), v_scales[0].bitcast(I32))
+
+        def load_x_scale_rows(n):
+            r, o = divmod(n, 2)
+            nc.sync.dma_start(x_bytes[4 * o + r : P : 32, :].bitcast(I32), x_scales[o, r::4, :].bitcast(I32))
+
+        for n in range(ROWS_AHEAD):
+            load_x_scale_rows(n)
         w_raw = [load_w(0)]
-        nc.sync.dma_start(v_bytes[0:P:8, :].bitcast(I32), v_scales[0].bitcast(I32))
+        for n in range(ROWS_AHEAD, 8):
+            load_x_scale_rows(n)
         w_raw.append(load_w(1))
         nc.sync.dma_start(x_table[1][:], words_of(x_words, 1))
         v_table = turns.tile([P, G], I32, name="v_table", align_bytes=64, offset=0)
@@ -105,13 +112,14 @@ def tile_picked_zmoco_relu_p_kernel(
             )
 
         gather_x(0, x0_codes[:], 0, CHUNKS)
-        nc.vector.tensor_copy(x_scale[:], x_bytes[:].indirect(offs_sb[:]))
-        for half in range(2):
-            nc.scalar.activation(dst[0][half], src[0][:, :, :, 2 * half : 2 * half + 2], ACT.Copy)
         nc.vector.tensor_copy(v_rows[:], v_bytes[:].indirect(neg_sb[:]))
+        nc.vector.tensor_copy(dst[0][0][:, : P // 2], src[0][:, : P // 2, :, :2])
+        nc.scalar.activation(dst[0][0][:, P // 2 :], src[0][:, P // 2 :, :, :2], ACT.Copy)
+        nc.scalar.activation(dst[0][1], src[0][:, :, :, 2:], ACT.Copy)
+        nc.vector.tensor_copy(x_scale[:], x_bytes[:].indirect(offs_sb[:]))
         for q in range(QUADS):
             nc.sync.dma_start(
-                v_scale[32 * q : 32 * q + 4, :].bitcast(I32), v_rows[32 * q : 32 * (q + 1) : 8, :].bitcast(I32)
+                v_scale[32 * q : 32 * q + 4, :].bitcast(I32), v_rows[V_ROWS_AT + 4 * q : V_ROWS_AT + 4 * q + 4, :].bitcast(I32)
             )
         quantize_w(0, 0)
         nc.vector.tensor_copy(dst[1][0], src[1][:, :, :, :2])

@@ -40,7 +40,7 @@ def tile_picked_zmoco_relu_p_kernel(
             return table[o].rearrange("p n r -> p (n r)").bitcast(I32)
 
         def load_w(o):
-            raw = sb.tile([P, PACK, H], F32, name=f"w_raw{o}")
+            raw = turns.tile([P, PACK, H], F32, name=f"w_raw{o}", offset=4 * G * (1 + o))
             nc.sync.dma_start(raw[:], w1[512 * o : 512 * (o + 1), :].rearrange("(p r) i -> p r i", r=PACK))
             return raw
 
@@ -73,21 +73,21 @@ def tile_picked_zmoco_relu_p_kernel(
         v_table = turns.tile([P, G], I32, name="v_table", align_bytes=64, offset=0)
         nc.sync.dma_start(v_table[:], words_of(v_words, 0))
 
-        spare = 4 * G
         x0_codes = sb.tile([P, S], U32, name="x0_codes", align_bytes=64)
         x1_first = sb.tile([P, CHUNK], U32, name="x1_first", align_bytes=64)
-        x1_rest = turns.tile([P, S - CHUNK], U32, name="x1_rest", align_bytes=64, offset=spare + 12 * S)
+        x1_rest = turns.tile([P, S - CHUNK], U32, name="x1_rest", align_bytes=64, offset=8 * G)
         x_codes = [
             [x0_codes[:, CHUNK * c : CHUNK * (c + 1)] for c in range(CHUNKS)],
             [x1_first[:]] + [x1_rest[:, CHUNK * c : CHUNK * (c + 1)] for c in range(CHUNKS - 1)],
         ]
         x_scale = sb.tile([P, S], U8, name="x_scale", align_bytes=64)
-        late = spare + 16 * S
-        v_rows = turns.tile([P, V], U8, name="v_rows", align_bytes=64, offset=late + 8 * S)
+        late = 12 * G
+        moved = late + 4 * CHUNK
+        v_rows = turns.tile([P, V], U8, name="v_rows", align_bytes=64, offset=moved)
 
         w_bf = [
             [
-                turns.tile([P, 2, P, PACK], BF16, name=f"w_bf{o}{half}", align_bytes=64, offset=spare + 4 * S * (2 * o + half))
+                sb.tile([P, 2, P, PACK], BF16, name=f"w_bf{o}{half}", align_bytes=64)
                 for half in range(2)
             ]
             for o in range(2)
@@ -150,10 +150,7 @@ def tile_picked_zmoco_relu_p_kernel(
         gather_x(1, x_codes[1][1], 1, 2)
         gather_x(1, x1_rest[:, CHUNK:], 2, 4)
 
-        h_bf = [
-            turns.tile([P, CHUNK, PACK], BF16, name=f"h_bf{c}", align_bytes=64, offset=late + 8 * CHUNK * c)
-            for c in range(CHUNKS)
-        ]
+        h_bf = [sb.tile([P, CHUNK, PACK], BF16, name=f"h_bf{c}", align_bytes=64) for c in range(CHUNKS)]
 
         def hidden(c):
             for j in range(PACK):
@@ -164,10 +161,15 @@ def tile_picked_zmoco_relu_p_kernel(
             hidden(c)
 
         h_codes = [
-            turns.tile([P, CHUNK], U32, name=f"h_codes{c}", align_bytes=64, offset=where)
-            for c, where in enumerate((late + 8 * S, 0, 4 * CHUNK, late + 8 * S))
+            turns.tile([P, CHUNK], U32, name="h_codes0", align_bytes=64, offset=late),
+            sb.tile([P, CHUNK], U32, name="h_codes1", align_bytes=64),
+            sb.tile([P, CHUNK], U32, name="h_codes2", align_bytes=64),
+            turns.tile([P, CHUNK], U32, name="h_codes3", align_bytes=64, offset=late),
         ]
-        h_scale = [sb.tile([P, CHUNK], U8, name=f"h_scale{c}", align_bytes=64) for c in range(CHUNKS)]
+        h_scale = [
+            turns.tile([P, CHUNK], U8, name=f"h_scale{c}", align_bytes=64, offset=moved + CHUNK * c)
+            for c in range(CHUNKS - 1)
+        ] + [sb.tile([P, CHUNK], U8, name="h_scale3", align_bytes=64)]
 
         def quantize_h(c):
             nc.vector.quantize_mx(
@@ -178,7 +180,7 @@ def tile_picked_zmoco_relu_p_kernel(
 
         v_codes = [
             sb.tile([P, V // 2], U32, name="v_codes0", align_bytes=64),
-            turns.tile([P, V // 2], U32, name="v_codes1", align_bytes=64, offset=late),
+            turns.tile([P, V // 2], U32, name="v_codes1", align_bytes=64, offset=moved + 3 * CHUNK),
         ]
 
         def gather_v(half):

@@ -21,7 +21,6 @@ QUADS = 4
 CHUNK = 128
 CHUNKS = S // CHUNK
 LIST_COLS = CHUNK // 16
-GPSIMD_CHUNKS = 1
 ROWS_AHEAD = 3
 V_ROWS_AT = 8
 
@@ -218,10 +217,7 @@ def tile_picked_zmoco_relu_p_kernel(
 
         def normalise(c):
             prob = sb.tile([P, V], F32, name=f"prob{c}")
-            if c < GPSIMD_CHUNKS:
-                nc.gpsimd.tensor_scalar(prob[:], e[c][:], inv[c][:], 0.0, ALU.mult, ALU.add)
-            else:
-                nc.vector.tensor_scalar(prob[:], e[c][:], inv[c][:], None, ALU.mult)
+            nc.vector.tensor_scalar(prob[:], e[c][:], inv[c][:], None, ALU.mult)
             nc.sync.dma_start(out[CHUNK * c : CHUNK * (c + 1), :], prob[:])
 
         exponentials(0)

@@ -43,20 +43,19 @@ def tile_picked_zmoco_relu_p_kernel(
             nc.sync.dma_start(raw[:], w1[512 * o : 512 * (o + 1), :].rearrange("(p r) i -> p r i", r=PACK))
             return raw
 
-        v_bytes = sb.tile([P, G], U8, name="v_bytes", align_bytes=64)
-        nc.vector.memset(v_bytes[:].bitcast(I32), 0)
         x_bytes = sb.tile([P, T], U8, name="x_bytes", align_bytes=64)
         nc.vector.memset(x_bytes[:].bitcast(I32), 0)
+        v_bytes = sb.tile([P, G], U8, name="v_bytes", align_bytes=64)
+        nc.vector.memset(v_bytes[:].bitcast(I32), 0)
         v_scale = sb.tile([P, V], U8, name="v_scale", align_bytes=64)
         nc.vector.memset(v_scale[:].bitcast(I32), 0)
 
         x_table = [sb.tile([P, T], I32, name=f"x_table{o}", align_bytes=64) for o in range(2)]
+        nc.sync.dma_start(x_table[0][:], words_of(x_words, 0))
         neg_sb = lists.tile([P, V // 16], U16, name="neg_sb")
         nc.sync.dma_start(neg_sb[:], neg)
-        nc.sync.dma_start(x_table[0][:], words_of(x_words, 0))
         offs_sb = lists.tile([P, S // 16], U16, name="offs_sb")
         nc.sync.dma_start(offs_sb[:], offs)
-        nc.sync.dma_start(v_bytes[V_ROWS_AT : V_ROWS_AT + 16, :].bitcast(I32), v_scales[0].bitcast(I32))
 
         def load_x_scale_rows(n):
             r, o = divmod(n, 2)
@@ -64,6 +63,7 @@ def tile_picked_zmoco_relu_p_kernel(
 
         for n in range(ROWS_AHEAD):
             load_x_scale_rows(n)
+        nc.sync.dma_start(v_bytes[V_ROWS_AT : V_ROWS_AT + 16, :].bitcast(I32), v_scales[0].bitcast(I32))
         w_raw = [load_w(0)]
         for n in range(ROWS_AHEAD, 8):
             load_x_scale_rows(n)

@@ -23,6 +23,7 @@ CHUNKS = S // CHUNK
 LIST_COLS = CHUNK // 16
 ROWS_AHEAD = 3
 V_ROWS_AT = 8
+V_EARLY = 384
 
 
 def tile_picked_zmoco_relu_p_kernel(
@@ -178,19 +179,14 @@ def tile_picked_zmoco_relu_p_kernel(
             )
 
         v_codes = [
-            sb.tile([P, V // 2], U32, name="v_codes0", align_bytes=64),
-            turns.tile([P, V // 2], U32, name="v_codes1", align_bytes=64, offset=moved + 3 * CHUNK),
+            sb.tile([P, V_EARLY], U32, name="v_codes0", align_bytes=64),
+            turns.tile([P, V - V_EARLY], U32, name="v_codes1", align_bytes=64, offset=moved + 3 * CHUNK),
         ]
 
-        def gather_v(half):
-            nc.vector.tensor_copy(
-                v_codes[half][:],
-                v_table[:].bitcast(U32).indirect(neg_sb[:, V // 32 * half : V // 32 * (half + 1)]),
-            )
-
-        gather_v(0)
+        nc.vector.tensor_copy(v_codes[0][:], v_table[:].bitcast(U32).indirect(neg_sb[:, : V_EARLY // 16]))
         quantize_h(0)
-        gather_v(1)
+        nc.vector.tensor_copy(v_codes[1][:], v_table[:].bitcast(U32).indirect(neg_sb[:, V_EARLY // 16 :]))
+        v_runs = [(v_codes[0][:, :256], 0, 256), (v_codes[0][:, 256:], 256, V_EARLY), (v_codes[1][:], V_EARLY, V)]
         for c in range(1, CHUNKS - 1):
             quantize_h(c)
 
@@ -198,13 +194,13 @@ def tile_picked_zmoco_relu_p_kernel(
         total = [sb.tile([P, 1], F32, name=f"total{c}") for c in range(CHUNKS)]
 
         def exponentials(c):
-            for half in range(2):
-                cols = slice(V // 2 * half, V // 2 * (half + 1))
+            for codes, first, last in v_runs:
+                cols = slice(first, last)
                 nc.tensor.matmul_mx(
                     out=y_acc[c][:, cols],
                     lhsT=h_codes[c][:].bitcast(FP8X4),
                     lhsT_scale=h_scale[c][:],
-                    rhs=v_codes[half][:].bitcast(FP8X4),
+                    rhs=codes.bitcast(FP8X4),
                     rhs_scale=v_scale[:, cols],
                     start=True,
                     stop=True,

@@ -22,7 +22,7 @@ CHUNK = 128
 CHUNKS = S // CHUNK
 LIST_COLS = CHUNK // 16
 ROWS_AHEAD = 3
-V_ROWS_AT = 8
+V_ROWS_AT = 32
 V_EARLY = 384
 
 
@@ -64,7 +64,7 @@ def tile_picked_zmoco_relu_p_kernel(
 
         for n in range(ROWS_AHEAD):
             load_x_scale_rows(n)
-        nc.sync.dma_start(v_bytes[V_ROWS_AT : V_ROWS_AT + 16, :].bitcast(I32), v_scales[0].bitcast(I32))
+        nc.sync.dma_start(v_bytes[V_ROWS_AT : V_ROWS_AT + 64 : 4, :].bitcast(I32), v_scales[0].bitcast(I32))
         w_raw = [load_w(0)]
         for n in range(ROWS_AHEAD, 8):
             load_x_scale_rows(n)
@@ -119,7 +119,7 @@ def tile_picked_zmoco_relu_p_kernel(
         nc.vector.tensor_copy(x_scale[:], x_bytes[:].indirect(offs_sb[:]))
         for q in range(QUADS):
             nc.sync.dma_start(
-                v_scale[32 * q : 32 * q + 4, :].bitcast(I32), v_rows[V_ROWS_AT + 4 * q : V_ROWS_AT + 4 * q + 4, :].bitcast(I32)
+                v_scale[32 * q : 32 * q + 4, :].bitcast(I32), v_rows[V_ROWS_AT + 16 * q : V_ROWS_AT + 16 * (q + 1) : 4, :].bitcast(I32)
             )
         quantize_w(0, 0)
         nc.vector.tensor_copy(dst[1][0], src[1][:, :, :, :2])

@@ -24,6 +24,7 @@ LIST_COLS = CHUNK // 16
 ROWS_AHEAD = 3
 V_ROWS_AT = 32
 V_EARLY = 384
+LAST_SPLIT = 352
 
 
 def tile_picked_zmoco_relu_p_kernel(
@@ -205,23 +206,36 @@ def tile_picked_zmoco_relu_p_kernel(
                     start=True,
                     stop=True,
                 )
-            neg_max = sb.tile([P, 1], F32, name=f"neg_max{c}")
+            if c == 2:
+                neg_max = turns.tile([P, 1], F32, name="neg_max2", align_bytes=64, offset=14 * G)
+            else:
+                neg_max = sb.tile([P, 1], F32, name=f"neg_max{c}")
             nc.vector.tensor_reduce(neg_max[:], y_acc[c][:], mybir.AxisListType.X, ALU.max, negate=True)
             nc.scalar.activation(e[c][:], y_acc[c][:], ACT.Exp, bias=neg_max[:], scale=1.0, accum_out=total[c][:])
 
         inv = [sb.tile([P, 1], F32, name=f"inv{c}") for c in range(CHUNKS)]
 
         def normalise(c):
-            prob = sb.tile([P, V], F32, name=f"prob{c}")
-            nc.vector.tensor_scalar(prob[:], e[c][:], inv[c][:], None, ALU.mult)
+            if c == 1:
+                prob = turns.tile([P, V], F32, name="prob1", align_bytes=64, offset=14 * G)
+            else:
+                prob = sb.tile([P, V], F32, name=f"prob{c}")
+            cut = LAST_SPLIT if c == CHUNKS - 1 else V
+            nc.vector.tensor_scalar(prob[:, :cut], e[c][:, :cut], inv[c][:], None, ALU.mult)
+            if cut < V:
+                nc.scalar.activation(prob[:, cut:], e[c][:, cut:], ACT.Copy, scale=inv[c][:])
             nc.sync.dma_start(out[CHUNK * c : CHUNK * (c + 1), :], prob[:])
 
         exponentials(0)
         quantize_h(CHUNKS - 1)
-        for c in range(1, CHUNKS):
+        for c in range(1, CHUNKS - 1):
             exponentials(c)
-            nc.vector.reciprocal(inv[c - 1][:], total[c - 1][:])
-        for c in range(CHUNKS - 1):
+        nc.vector.reciprocal(inv[0][:], total[0][:])
+        exponentials(CHUNKS - 1)
+        normalise(0)
+        for c in range(1, CHUNKS - 1):
+            nc.vector.reciprocal(inv[c][:], total[c][:])
+        for c in range(1, CHUNKS - 1):
             normalise(c)
         nc.vector.reciprocal(inv[CHUNKS - 1][:], total[CHUNKS - 1][:])
         normalise(CHUNKS - 1)

@@ -118,9 +118,9 @@ def tile_picked_zmoco_relu_p_kernel(
         nc.scalar.activation(dst[0][0][:, P // 2 :], src[0][:, P // 2 :, :, :2], ACT.Copy)
         nc.scalar.activation(dst[0][1], src[0][:, :, :, 2:], ACT.Copy)
         nc.vector.tensor_copy(x_scale[:], x_bytes[:].indirect(offs_sb[:]))
-        for q in range(QUADS):
+        for r in range(4):
             nc.sync.dma_start(
-                v_scale[32 * q : 32 * q + 4, :].bitcast(I32), v_rows[V_ROWS_AT + 16 * q : V_ROWS_AT + 16 * (q + 1) : 4, :].bitcast(I32)
+                v_scale[r:P:32, :].bitcast(I32), v_rows[V_ROWS_AT + 4 * r : V_ROWS_AT + 64 : 16, :].bitcast(I32)
             )
         quantize_w(0, 0)
         nc.vector.tensor_copy(dst[1][0], src[1][:, :, :, :2])
@@ -220,7 +220,7 @@ def tile_picked_zmoco_relu_p_kernel(
                 prob = turns.tile([P, V], F32, name="prob1", align_bytes=64, offset=14 * G)
             else:
                 prob = sb.tile([P, V], F32, name=f"prob{c}")
-            cut = LAST_SPLIT if c == CHUNKS - 1 else V
+            cut = LAST_SPLIT if c >= CHUNKS - 2 else V
             nc.vector.tensor_scalar(prob[:, :cut], e[c][:, :cut], inv[c][:], None, ALU.mult)
             if cut < V:
                 nc.scalar.activation(prob[:, cut:], e[c][:, cut:], ACT.Copy, scale=inv[c][:])

from contextlib import ExitStack

import concourse.mybir as mybir

K, T, S, V, H, G = 1024, 1024, 512, 512, 512, 2048
FLOPS = 2 * K * H * S + 2 * H * S * V

F32 = mybir.dt.float32
BF16 = mybir.dt.bfloat16
I32 = mybir.dt.int32
U32 = mybir.dt.uint32
U16 = mybir.dt.uint16
U8 = mybir.dt.uint8
FP8X4 = mybir.dt.float8_e4m3fn_x4
ACT = mybir.ActivationFunctionType
ALU = mybir.AluOpType

P = 128
PACK = 4
QUADS = 4
CHUNK = 128
CHUNKS = S // CHUNK
LIST_COLS = CHUNK // 16
ROWS_AHEAD = 3
V_ROWS_AT = 32
V_EARLY = 384
LAST_SPLIT = 352


def tile_picked_zmoco_relu_p_kernel(
    tc, x_words, x_scales, w1, v_words, v_scales, offs, neg, out
):
    nc = tc.nc
    with ExitStack() as ctx:
        lists = ctx.enter_context(tc.tile_pool(name="lists", bufs=1))
        sb = ctx.enter_context(tc.tile_pool(name="sb", bufs=1))
        turns = ctx.enter_context(tc.tile_pool(name="turns", bufs=1))
        psum = ctx.enter_context(tc.psum_pool(name="psum", bufs=1))

        def words_of(table, o):
            return table[o].rearrange("p n r -> p (n r)").bitcast(I32)

        def load_w(o):
            raw = turns.tile([P, PACK, H], F32, name=f"w_raw{o}", offset=4 * G * (1 + o))
            nc.sync.dma_start(raw[:], w1[512 * o : 512 * (o + 1), :].rearrange("(p r) i -> p r i", r=PACK))
            return raw

        x_bytes = sb.tile([P, T], U8, name="x_bytes", align_bytes=64)
        nc.vector.memset(x_bytes[:].bitcast(I32), 0)
        v_bytes = sb.tile([P, G], U8, name="v_bytes", align_bytes=64)
        nc.vector.memset(v_bytes[:].bitcast(I32), 0)
        v_scale = sb.tile([P, V], U8, name="v_scale", align_bytes=64)
        nc.vector.memset(v_scale[:].bitcast(I32), 0)

        x_table = [sb.tile([P, T], I32, name=f"x_table{o}", align_bytes=64) for o in range(2)]
        nc.sync.dma_start(x_table[0][:], words_of(x_words, 0))
        neg_sb = lists.tile([P, V // 16], U16, name="neg_sb")
        nc.sync.dma_start(neg_sb[:], neg)
        offs_sb = lists.tile([P, S // 16], U16, name="offs_sb")
        nc.sync.dma_start(offs_sb[:], offs)

        def load_x_scale_rows(n):
            r, o = divmod(n, 2)
            nc.sync.dma_start(x_bytes[4 * o + r : P : 32, :].bitcast(I32), x_scales[o, r::4, :].bitcast(I32))

        for n in range(ROWS_AHEAD):
            load_x_scale_rows(n)
        nc.sync.dma_start(v_bytes[V_ROWS_AT : V_ROWS_AT + 64 : 4, :].bitcast(I32), v_scales[0].bitcast(I32))
        w_raw = [load_w(0)]
        for n in range(ROWS_AHEAD, 8):
            load_x_scale_rows(n)
        w_raw.append(load_w(1))
        nc.sync.dma_start(x_table[1][:], words_of(x_words, 1))
        v_table = turns.tile([P, G], I32, name="v_table", align_bytes=64, offset=0)
        nc.sync.dma_start(v_table[:], words_of(v_words, 0))

        x0_codes = sb.tile([P, S], U32, name="x0_codes", align_bytes=64)
        x1_first = sb.tile([P, CHUNK], U32, name="x1_first", align_bytes=64)
        x1_rest = turns.tile([P, S - CHUNK], U32, name="x1_rest", align_bytes=64, offset=8 * G)
        x_codes = [
            [x0_codes[:, CHUNK * c : CHUNK * (c + 1)] for c in range(CHUNKS)],
            [x1_first[:]] + [x1_rest[:, CHUNK * c : CHUNK * (c + 1)] for c in range(CHUNKS - 1)],
        ]
        x_scale = sb.tile([P, S], U8, name="x_scale", align_bytes=64)
        late = 12 * G
        moved = late + 4 * CHUNK
        v_rows = turns.tile([P, V], U8, name="v_rows", align_bytes=64, offset=moved)

        w_bf = [
            [
                sb.tile([P, 2, P, PACK], BF16, name=f"w_bf{o}{half}", align_bytes=64)
                for half in range(2)
            ]
            for o in range(2)
        ]
        w_codes = [sb.tile([P, H], U32, name=f"w_codes{o}", align_bytes=64) for o in range(2)]
        w_scale = [sb.tile([P, H], U8, name=f"w_scale{o}", align_bytes=64) for o in range(2)]
        src = [w_raw[o][:].rearrange("p r (m j) -> p m r j", j=PACK) for o in range(2)]
        dst = [[w_bf[o][half][:].rearrange("p j m r -> p m r j") for half in range(2)] for o in range(2)]

        def quantize_w(o, half):
            cols = slice(2 * P * half, 2 * P * (half + 1))
            nc.vector.quantize_mx(
                out=w_codes[o][:, cols].bitcast(FP8X4),
                scales=w_scale[o][:, cols],
                in_=w_bf[o][half][:].rearrange("p j m r -> p (j m r)"),
            )

        def gather_x(o, codes, c0, c1):
            nc.vector.tensor_copy(
                codes,
                x_table[o][:].bitcast(U32).indirect(offs_sb[:, LIST_COLS * c0 : LIST_COLS * c1]),
            )

        gather_x(0, x0_codes[:], 0, CHUNKS)
        nc.vector.tensor_copy(v_rows[:], v_bytes[:].indirect(neg_sb[:]))
        nc.vector.tensor_copy(dst[0][0][:, : P // 2], src[0][:, : P // 2, :, :2])
        nc.scalar.activation(dst[0][0][:, P // 2 :], src[0][:, P // 2 :, :, :2], ACT.Copy)
        nc.scalar.activation(dst[0][1], src[0][:, :, :, 2:], ACT.Copy)
        nc.vector.tensor_copy(x_scale[:], x_bytes[:].indirect(offs_sb[:]))
        for r in range(4):
            nc.sync.dma_start(
                v_scale[r:P:32, :].bitcast(I32), v_rows[V_ROWS_AT + 4 * r : V_ROWS_AT + 64 : 16, :].bitcast(I32)
            )
        quantize_w(0, 0)
        nc.vector.tensor_copy(dst[1][0], src[1][:, :, :, :2])
        nc.scalar.activation(dst[1][1], src[1][:, :, :, 2:], ACT.Copy)
        quantize_w(0, 1)

        y_acc = [psum.tile([P, V], F32, name=f"y_acc{c}") for c in range(CHUNKS)]
        h_acc = [psum.tile([P, PACK, CHUNK], F32, name=f"h_acc{c}") for c in range(CHUNKS)]

        def hidden_pass(c, j, o):
            nc.tensor.matmul_mx(
                out=h_acc[c][:, j, :],
                lhsT=w_codes[o][:, P * j : P * (j + 1)].bitcast(FP8X4),
                lhsT_scale=w_scale[o][:, P * j : P * (j + 1)],
                rhs=x_codes[o][c].bitcast(FP8X4),
                rhs_scale=x_scale[4 * o :, CHUNK * c : CHUNK * (c + 1)],
                start=(o == 0 and j == 0),
                stop=(o == 1 and j == PACK - 1),
            )

        for half in range(2):
            for c in range(CHUNKS):
                for j in range(2):
                    hidden_pass(c, 2 * half + j, 0)
        quantize_w(1, 0)
        gather_x(1, x_codes[1][0], 0, 1)
        quantize_w(1, 1)
        gather_x(1, x_codes[1][1], 1, 2)
        gather_x(1, x1_rest[:, CHUNK:], 2, 4)

        h_bf = [sb.tile([P, CHUNK, PACK], BF16, name=f"h_bf{c}", align_bytes=64) for c in range(CHUNKS)]

        def hidden(c):
            for j in range(PACK):
                hidden_pass(c, j, 1)
            nc.scalar.activation(h_bf[c][:], h_acc[c][:].rearrange("p j t -> p t j"), ACT.Relu)

        for c in range(CHUNKS):
            hidden(c)

        h_codes = [
            turns.tile([P, CHUNK], U32, name="h_codes0", align_bytes=64, offset=late),
            sb.tile([P, CHUNK], U32, name="h_codes1", align_bytes=64),
            sb.tile([P, CHUNK], U32, name="h_codes2", align_bytes=64),
            turns.tile([P, CHUNK], U32, name="h_codes3", align_bytes=64, offset=late),
        ]
        h_scale = [
            turns.tile([P, CHUNK], U8, name=f"h_scale{c}", align_bytes=64, offset=moved + CHUNK * c)
            for c in range(CHUNKS - 1)
        ] + [sb.tile([P, CHUNK], U8, name="h_scale3", align_bytes=64)]

        def quantize_h(c):
            nc.vector.quantize_mx(
                out=h_codes[c][:].bitcast(FP8X4),
                scales=h_scale[c][:],
                in_=h_bf[c][:].rearrange("p t j -> p (t j)"),
            )

        v_codes = [
            sb.tile([P, V_EARLY], U32, name="v_codes0", align_bytes=64),
            turns.tile([P, V - V_EARLY], U32, name="v_codes1", align_bytes=64, offset=moved + 3 * CHUNK),
        ]

        nc.vector.tensor_copy(v_codes[0][:], v_table[:].bitcast(U32).indirect(neg_sb[:, : V_EARLY // 16]))
        quantize_h(0)
        nc.vector.tensor_copy(v_codes[1][:], v_table[:].bitcast(U32).indirect(neg_sb[:, V_EARLY // 16 :]))
        v_runs = [(v_codes[0][:, :256], 0, 256), (v_codes[0][:, 256:], 256, V_EARLY), (v_codes[1][:], V_EARLY, V)]
        for c in range(1, CHUNKS - 1):
            quantize_h(c)

        e = [sb.tile([P, V], F32, name=f"e{c}") for c in range(CHUNKS)]
        total = [sb.tile([P, 1], F32, name=f"total{c}") for c in range(CHUNKS)]

        def exponentials(c):
            for codes, first, last in v_runs:
                cols = slice(first, last)
                nc.tensor.matmul_mx(
                    out=y_acc[c][:, cols],
                    lhsT=h_codes[c][:].bitcast(FP8X4),
                    lhsT_scale=h_scale[c][:],
                    rhs=codes.bitcast(FP8X4),
                    rhs_scale=v_scale[:, cols],
                    start=True,
                    stop=True,
                )
            if c == 2:
                neg_max = turns.tile([P, 1], F32, name="neg_max2", align_bytes=64, offset=14 * G)
            else:
                neg_max = sb.tile([P, 1], F32, name=f"neg_max{c}")
            nc.vector.tensor_reduce(neg_max[:], y_acc[c][:], mybir.AxisListType.X, ALU.max, negate=True)
            nc.scalar.activation(e[c][:], y_acc[c][:], ACT.Exp, bias=neg_max[:], scale=1.0, accum_out=total[c][:])

        inv = [sb.tile([P, 1], F32, name=f"inv{c}") for c in range(CHUNKS)]

        def normalise(c):
            if c == 1:
                prob = turns.tile([P, V], F32, name="prob1", align_bytes=64, offset=14 * G)
            else:
                prob = sb.tile([P, V], F32, name=f"prob{c}")
            cut = LAST_SPLIT if c >= CHUNKS - 2 else V
            nc.vector.tensor_scalar(prob[:, :cut], e[c][:, :cut], inv[c][:], None, ALU.mult)
            if cut < V:
                nc.scalar.activation(prob[:, cut:], e[c][:, cut:], ACT.Copy, scale=inv[c][:])
            nc.sync.dma_start(out[CHUNK * c : CHUNK * (c + 1), :], prob[:])

        exponentials(0)
        quantize_h(CHUNKS - 1)
        for c in range(1, CHUNKS - 1):
            exponentials(c)
        nc.vector.reciprocal(inv[0][:], total[0][:])
        exponentials(CHUNKS - 1)
        normalise(0)
        for c in range(1, CHUNKS - 1):
            nc.vector.reciprocal(inv[c][:], total[c][:])
        for c in range(1, CHUNKS - 1):
            normalise(c)
        nc.vector.reciprocal(inv[CHUNKS - 1][:], total[CHUNKS - 1][:])
        normalise(CHUNKS - 1)
